import numpy as np
import ml_dtypes


def mxq(x, axis, fmt="e4m3"):
    dtype, down = {"e4m3": (ml_dtypes.float8_e4m3fn, 7), "e5m2": (ml_dtypes.float8_e5m2, 14)}[fmt]
    v = np.moveaxis(np.asarray(x, np.float32).astype(ml_dtypes.bfloat16).astype(np.float64), axis, -1)
    blocks = v.reshape(v.shape[:-1] + (-1, 32))
    amax = np.abs(blocks).max(-1, keepdims=True)
    byte = np.maximum(np.where(amax > 0, np.frexp(amax)[1] - 1 + 127, 0) - down, 1)
    scale = np.exp2(byte - 127.0)
    codes = (blocks / scale).astype(np.float32).astype(dtype).astype(np.float64)
    return np.moveaxis((codes * scale).reshape(v.shape), -1, axis)


WIDE = False


def mx_kscale(k):
    if not WIDE:
        return np.ones(k)
    levels = np.array([10, -10, 5, -5, 0])
    if k % 512:
        return np.exp2(np.random.permutation(np.resize(levels, k // 32))).repeat(32)
    a = np.empty((k // 512, 16))
    for p in range(k // 512):
        a[p, :8] = np.random.permutation(np.resize(levels, 8))
        for g in range(8):
            far = levels[np.abs(levels - a[p, g]) >= 10]
            a[p, g + 8] = far[np.random.randint(len(far))]
    return np.exp2(a.ravel()).repeat(32)


def f64(x):
    return np.asarray(x).astype(np.float64)


def striped(idx):
    return np.tile(np.asarray(idx).reshape(-1, 16).T, (8, 1)).astype(np.uint16)


def unstriped(offs):
    return offs[:16].T.reshape(-1).astype(np.int64)


E2M1 = np.array([0.0, 0.5, 1.0, 1.5, 2.0, 3.0, 4.0, 6.0, -0.0, -0.5, -1.0, -1.5, -2.0, -3.0, -4.0, -6.0])


def pack_weight(w, fmt):
    k, n = w.shape
    w = f64(np.asarray(w, np.float32).astype(ml_dtypes.bfloat16)).reshape(k // 32, 32, n)
    amax = np.abs(w).max(1)
    if fmt == "e4m3":
        byte = np.frexp(amax)[1] - 1 + 127 - 7
    else:
        mant, ex = np.frexp(amax / 6.0)
        byte = np.where(mant > 0.5, ex, ex - 1) + 127
    byte = np.clip(np.where(amax > 0, byte, 1), 1, 254)
    scaled = (w * np.exp2(127.0 - byte)[:, None, :]).reshape(k, n).astype(np.float32)
    by_word = np.ascontiguousarray(scaled.reshape(k // 512, 128, 4, n).transpose(0, 1, 3, 2))
    if fmt == "e4m3":
        words = by_word.astype(ml_dtypes.float8_e4m3fn).view(np.uint8)
    else:
        c = by_word.astype(ml_dtypes.float4_e2m1fn).view(np.uint8) & 0xF
        words = (c[..., 0::2] | (c[..., 1::2] << 4)).reshape(k // 512, 128, 2 * n)
    return np.ascontiguousarray(words), np.ascontiguousarray(byte.astype(np.uint8).reshape(k // 512, 16, n))


def unpack_weight(words, scales, fmt):
    g, _, n = scales.shape
    words = np.ascontiguousarray(words).reshape(g, 128, n, -1)
    if fmt == "e4m3":
        vals = words.view(ml_dtypes.float8_e4m3fn).astype(np.float64)
    else:
        nib = np.empty((g, 128, n, 4), np.uint8)
        nib[..., 0::2] = words & 0xF
        nib[..., 1::2] = words >> 4
        vals = E2M1[nib]
    vals = vals * np.repeat(np.exp2(scales.astype(np.float64) - 127.0), 8, axis=1)[..., None]
    return vals.transpose(0, 1, 3, 2).reshape(g * 512, n)


def softplus(v):
    return np.log(1.0 + np.exp(v))


def sigmoid(v):
    return 1.0 / (1.0 + np.exp(-v))


K, R, F, T, J, M = 512, 128, 512, 2048, 512, 256


def setup_inputs():
    n = np.random.standard_normal
    idx = np.random.permutation(T)[:J]
    idx2 = np.random.permutation(J)[:M]
    idx3 = np.random.permutation(J)[:M]
    idx4 = np.random.permutation(J)[:M]
    fk = mx_kscale(K)
    dtabp = pack_weight(n((K, T)) / fk[:, None], "e2m1")
    tabp = pack_weight(n((K, T)) / fk[:, None], "e2m1")
    return {
        "dtab_words": dtabp[0],
        "dtab_scales": dtabp[1],
        "tab_words": tabp[0],
        "tab_scales": tabp[1],
        "w1": (n((K, R)) * 1 / np.sqrt(K) * fk[:, None]).astype(np.float32),
        "bias": (np.random.uniform(-0.5, 0.5, (R, 1))).astype(np.float32),
        "og": (np.random.uniform(0.5, 2.0, (R, 1))).astype(np.float32),
        "base": (0.3 * n((R, M))).astype(np.float32),
        "offs": striped(idx),
        "offs2": striped(idx2),
        "offs3": striped(idx3),
        "offs4": striped(idx4),
    }


def reference(dtab_words, dtab_scales, tab_words, tab_scales, w1, bias, og, base, offs, offs2, offs3, offs4):
    idx = unstriped(offs)
    idx2 = unstriped(offs2)
    idx3 = unstriped(offs3)
    idx4 = unstriped(offs4)
    dtabu = unpack_weight(dtab_words, dtab_scales, "e2m1")
    tabu = unpack_weight(tab_words, tab_scales, "e2m1")
    w1q = mxq(f64(w1), 0, "e4m3")
    tabidxg = tabu[:, idx]
    a = w1q.T @ tabidxg
    dtabidxg = dtabu[:, idx]
    ta = w1q.T @ dtabidxg
    h1 = softplus(a + f64(bias))
    s = h1[:, idx2] * h1[:, idx3] * h1[:, idx4]
    th1 = ta * sigmoid(a + f64(bias))
    ts = (th1[:, idx2] * h1[:, idx3] + th1[:, idx3] * h1[:, idx2]) * h1[:, idx4] + th1[:, idx4] * h1[:, idx2] * h1[:, idx3]
    tu1 = ts / (s + 1.0)
    y = tu1 * f64(og) + f64(base)
    return y

@@ -1,0 +1,154 @@
+from contextlib import ExitStack
+
+import concourse.mybir as mybir
+
+F32 = mybir.dt.float32
+BF16 = mybir.dt.bfloat16
+I32 = mybir.dt.int32
+U32 = mybir.dt.uint32
+U16 = mybir.dt.uint16
+U8 = mybir.dt.uint8
+FP8X4 = mybir.dt.float8_e4m3fn_x4
+FP4X4 = mybir.dt.float4_e2m1fn_x4
+ACT = mybir.ActivationFunctionType
+ALU = mybir.AluOpType
+
+K, R, T, J, M = 512, 128, 2048, 512, 256
+P = 128
+PACK = 4
+HALF = J // 2
+CLAMP = 24.0
+FLOPS = 2 * 2 * K * R * J
+
+
+def tile_attend_ttriples_kernel(tc, dtab_words, dtab_scales, tab_words, tab_scales, w1, bias, og, base,
+                                 offs, offs2, offs3, offs4, out):
+    nc = tc.nc
+    with ExitStack() as ctx:
+        keep = ctx.enter_context(tc.tile_pool(name="keep", bufs=1))
+        psum = ctx.enter_context(tc.psum_pool(name="psum", bufs=1))
+
+        slots = keep.tile([P, J // 16], U16, name="slots")
+        first = keep.tile([P, M // 16], U16, name="first")
+        second = keep.tile([P, M // 16], U16, name="second")
+        third = keep.tile([P, M // 16], U16, name="third")
+        tab_s = keep.tile([P, T], U8, name="tab_s", align_bytes=64)
+        dtab_s = keep.tile([P, T], U8, name="dtab_s", align_bytes=64)
+        tab_w = keep.tile([P, T], U16, name="tab_w", align_bytes=64)
+
+        w_raw = keep.tile([P, PACK, R], F32, name="w_raw", tag="w_then_base")
+        bias_t = keep.tile([P, 1], F32, name="bias_t")
+        og_t = keep.tile([P, 1], F32, name="og_t")
+
+
+        def load_scales(tile, src):
+            rows = src[0].bitcast(I32).rearrange("(q r) c -> r q c", r=PACK)
+            view = tile[:].bitcast(I32)
+            for r in range(PACK):
+                nc.sync.dma_start(out=view[r:P:32, :], in_=rows[r])
+
+        nc.vector.memset(tab_s[:].bitcast(I32), 0)
+        nc.vector.memset(dtab_s[:].bitcast(I32), 0)
+        warm_in = keep.tile([P, 1], F32, name="warm_in", tag="warm_then_dtab", align_bytes=64)
+        warm_out = keep.tile([P, 1], F32, name="warm_out")
+        nc.gpsimd.memset(warm_in[:], 0.0)
+        nc.scalar.activation(warm_out[:], warm_in[:], ACT.Sigmoid)
+        dtab_w = keep.tile([P, T], U16, name="dtab_w", tag="warm_then_dtab", align_bytes=64)
+        nc.sync.dma_start(slots[:], offs)
+        nc.sync.dma_start(out=tab_w[:].bitcast(I32), in_=tab_words[0].bitcast(I32))
+        nc.sync.dma_start(out=w_raw[:], in_=w1.rearrange("(p j) r -> p j r", j=PACK))
+        load_scales(tab_s, tab_scales)
+        nc.gpsimd.dma_start(out=bias_t[:], in_=bias)
+        nc.gpsimd.dma_start(out=og_t[:], in_=og)
+        nc.sync.dma_start(out=dtab_w[:].bitcast(I32), in_=dtab_words[0].bitcast(I32))
+        load_scales(dtab_s, dtab_scales)
+        nc.sync.dma_start(first[:], offs2)
+        nc.sync.dma_start(second[:], offs3)
+        nc.sync.dma_start(third[:], offs4)
+
+        shifted = keep.tile([P, 1], F32, name="shifted")
+        nc.gpsimd.tensor_scalar(shifted[:], bias_t[:], 1.0, CLAMP, ALU.mult, ALU.add)
+
+        w_bf = keep.tile([P, R, PACK], BF16, name="w_bf", align_bytes=64)
+        nc.scalar.copy(w_bf[:], w_raw[:].rearrange("p j r -> p r j"))
+        base_t = keep.tile([P, M], F32, name="base_t", tag="w_then_base")
+        nc.sync.dma_start(out=base_t[:], in_=base)
+        w_codes = keep.tile([P, R], U32, name="w_codes", align_bytes=64)
+        w_scales = keep.tile([P, R], U8, name="w_scales", align_bytes=64)
+
+        def gather_words(name, window):
+            g = keep.tile([P, J], U16, name=name, tag=name, align_bytes=64)
+            nc.vector.tensor_copy(g[:], window[:].indirect(slots[:]))
+            return g
+
+        def gather_scales(name, window, half):
+            g = keep.tile([P, HALF], U8, name=name, align_bytes=64)
+            c = HALF // 16
+            nc.vector.tensor_copy(g[:], window[:].indirect(slots[:, half * c:(half + 1) * c]))
+            return g
+
+        def product(name, words, scales, half):
+            acc = psum.tile([P, HALF], F32, name=name)
+            nc.tensor.matmul_mx(out=acc[:], lhsT=w_codes[:].bitcast(FP8X4), lhsT_scale=w_scales[:],
+                                rhs=words[:, half * HALF:(half + 1) * HALF].bitcast(FP4X4), rhs_scale=scales[:],
+                                start=True, stop=True)
+            return acc
+
+        tab_wg = gather_words("tab_wg", tab_w)
+        tab_sg0 = gather_scales("tab_sg0", tab_s, 0)
+        nc.vector.quantize_mx(out=w_codes[:].bitcast(FP8X4), scales=w_scales[:],
+                              in_=w_bf[:].rearrange("p r j -> p (r j)"))
+        tab_sg = [tab_sg0, gather_scales("tab_sg1", tab_s, 1)]
+        lifted = keep.tile([P, J], F32, name="lifted")
+        sig = keep.tile([P, J], F32, name="sig")
+        for half in range(2):
+            cols = slice(half * HALF, (half + 1) * HALF)
+            a = product("a%d" % half, tab_wg, tab_sg[half], half)
+            nc.scalar.activation(lifted[:, cols], a[:], ACT.Relu, bias=shifted[:])
+            nc.scalar.activation(sig[:, cols], lifted[:, cols], ACT.Sigmoid, bias=-CLAMP)
+
+        dtab_wg = gather_words("dtab_wg", dtab_w)
+        tas = [product("ta%d" % half, dtab_wg, gather_scales("dtab_sg%d" % half, dtab_s, half), half) for half in range(2)]
+        th = keep.tile([P, J], F32, name="th")
+        for half in range(2):
+            cols = slice(half * HALF, (half + 1) * HALF)
+            nc.vector.tensor_tensor(th[:, cols], tas[half][:], sig[:, cols], ALU.mult)
+        th2 = keep.tile([P, M], F32, name="th2")
+        nc.vector.tensor_copy(th2[:], th[:].indirect(first[:]))
+
+        logsig = keep.tile([P, J], F32, name="logsig")
+        h = keep.tile([P, J], F32, name="h", tag="dtab_wg", align_bytes=64)
+        for half in range(2):
+            cols = slice(half * HALF, (half + 1) * HALF)
+            nc.scalar.activation(logsig[:, cols], sig[:, cols], ACT.Ln)
+            nc.vector.scalar_tensor_tensor(h[:, cols], lifted[:, cols], -CLAMP, logsig[:, cols], ALU.add, ALU.subtract)
+
+        def fresh(name):
+            return keep.tile([P, M], F32, name=name)
+
+        def times(name, window, offsets, other):
+            o = fresh(name)
+            nc.vector.tensor_tensor(o[:], window[:].indirect(offsets[:]), other[:], ALU.mult)
+            return o
+
+        h2 = fresh("h2")
+        nc.vector.tensor_copy(h2[:], h[:].indirect(first[:]))
+        u = times("u", h, second, th2)
+        pair = times("pair", h, second, h2)
+        v = times("v", th, second, h2)
+        s = times("s", h, third, pair)
+        root = fresh("root")
+        rec = fresh("rec")
+        nc.scalar.activation(root[:], s[:], ACT.Abs_reciprocal_sqrt, bias=1.0)
+        nc.scalar.activation(rec[:], root[:], ACT.Square)
+        w = fresh("w")
+        nc.vector.tensor_tensor(w[:], u[:], v[:], ALU.add)
+        y = times("y", th, third, pair)
+        x = times("x", h, third, w)
+        ts = fresh("ts")
+        nc.vector.tensor_tensor(ts[:], x[:], y[:], ALU.add)
+        scaled = fresh("scaled")
+        nc.vector.scalar_tensor_tensor(scaled[:], ts[:], og_t[:], rec[:], ALU.mult, ALU.mult)
+        res = fresh("res")
+        nc.vector.tensor_tensor(res[:], scaled[:], base_t[:], ALU.add)
+        nc.sync.dma_start(out=out, in_=res[:])

@@ -18,6 +18,7 @@ P = 128
 PACK = 4
 HALF = J // 2
 CLAMP = 24.0
+PARTS = 4
 FLOPS = 2 * 2 * K * R * J
 
 
@@ -33,7 +34,6 @@ def tile_attend_ttriples_kernel(tc, dtab_words, dtab_scales, tab_words, tab_scal
         second = keep.tile([P, M // 16], U16, name="second")
         third = keep.tile([P, M // 16], U16, name="third")
         tab_s = keep.tile([P, T], U8, name="tab_s", align_bytes=64)
-        dtab_s = keep.tile([P, T], U8, name="dtab_s", align_bytes=64)
         tab_w = keep.tile([P, T], U16, name="tab_w", align_bytes=64)
 
         w_raw = keep.tile([P, PACK, R], F32, name="w_raw", tag="w_then_base")
@@ -48,13 +48,15 @@ def tile_attend_ttriples_kernel(tc, dtab_words, dtab_scales, tab_words, tab_scal
                 nc.sync.dma_start(out=view[r:P:32, :], in_=rows[r])
 
         nc.vector.memset(tab_s[:].bitcast(I32), 0)
-        nc.vector.memset(dtab_s[:].bitcast(I32), 0)
         warm_in = keep.tile([P, 1], F32, name="warm_in", tag="warm_then_dtab", align_bytes=64)
-        warm_out = keep.tile([P, 1], F32, name="warm_out")
+        warm_out = keep.tile([P, 1], F32, name="warm_out", tag="warm_then_dscales", align_bytes=64)
         nc.gpsimd.memset(warm_in[:], 0.0)
         nc.scalar.activation(warm_out[:], warm_in[:], ACT.Sigmoid)
         dtab_w = keep.tile([P, T], U16, name="dtab_w", tag="warm_then_dtab", align_bytes=64)
+        dtab_s = keep.tile([P, T], U8, name="dtab_s", tag="warm_then_dscales", align_bytes=64)
+        nc.vector.memset(dtab_s[:].bitcast(I32), 0)
         nc.sync.dma_start(slots[:], offs)
+        nc.sync.dma_start(first[:], offs2)
         nc.sync.dma_start(out=tab_w[:].bitcast(I32), in_=tab_words[0].bitcast(I32))
         nc.sync.dma_start(out=w_raw[:], in_=w1.rearrange("(p j) r -> p j r", j=PACK))
         load_scales(tab_s, tab_scales)
@@ -62,7 +64,6 @@ def tile_attend_ttriples_kernel(tc, dtab_words, dtab_scales, tab_words, tab_scal
         nc.gpsimd.dma_start(out=og_t[:], in_=og)
         nc.sync.dma_start(out=dtab_w[:].bitcast(I32), in_=dtab_words[0].bitcast(I32))
         load_scales(dtab_s, dtab_scales)
-        nc.sync.dma_start(first[:], offs2)
         nc.sync.dma_start(second[:], offs3)
         nc.sync.dma_start(third[:], offs4)
 
@@ -113,8 +114,6 @@ def tile_attend_ttriples_kernel(tc, dtab_words, dtab_scales, tab_words, tab_scal
         for half in range(2):
             cols = slice(half * HALF, (half + 1) * HALF)
             nc.vector.tensor_tensor(th[:, cols], tas[half][:], sig[:, cols], ALU.mult)
-        th2 = keep.tile([P, M], F32, name="th2")
-        nc.vector.tensor_copy(th2[:], th[:].indirect(first[:]))
 
         logsig = keep.tile([P, J], F32, name="logsig")
         h = keep.tile([P, J], F32, name="h", tag="dtab_wg", align_bytes=64)
@@ -133,10 +132,16 @@ def tile_attend_ttriples_kernel(tc, dtab_words, dtab_scales, tab_words, tab_scal
 
         h2 = fresh("h2")
         nc.vector.tensor_copy(h2[:], h[:].indirect(first[:]))
-        u = times("u", h, second, th2)
-        pair = times("pair", h, second, h2)
+        h3 = fresh("h3")
+        nc.vector.tensor_copy(h3[:], h[:].indirect(second[:]))
         v = times("v", th, second, h2)
-        s = times("s", h, third, pair)
+        pair = fresh("pair")
+        nc.vector.tensor_tensor(pair[:], h2[:], h3[:], ALU.mult)
+        h4 = fresh("h4")
+        nc.vector.tensor_copy(h4[:], h[:].indirect(third[:]))
+        u = times("u", th, first, h3)
+        s = fresh("s")
+        nc.vector.tensor_tensor(s[:], pair[:], h4[:], ALU.mult)
         root = fresh("root")
         rec = fresh("rec")
         nc.scalar.activation(root[:], s[:], ACT.Abs_reciprocal_sqrt, bias=1.0)
@@ -144,11 +149,18 @@ def tile_attend_ttriples_kernel(tc, dtab_words, dtab_scales, tab_words, tab_scal
         w = fresh("w")
         nc.vector.tensor_tensor(w[:], u[:], v[:], ALU.add)
         y = times("y", th, third, pair)
-        x = times("x", h, third, w)
+        x = fresh("x")
         ts = fresh("ts")
-        nc.vector.tensor_tensor(ts[:], x[:], y[:], ALU.add)
         scaled = fresh("scaled")
-        nc.vector.scalar_tensor_tensor(scaled[:], ts[:], og_t[:], rec[:], ALU.mult, ALU.mult)
         res = fresh("res")
-        nc.vector.tensor_tensor(res[:], scaled[:], base_t[:], ALU.add)
-        nc.sync.dma_start(out=out, in_=res[:])
+        parts = [slice(q * M // PARTS, (q + 1) * M // PARTS) for q in range(PARTS)]
+        for c in parts:
+            nc.vector.tensor_tensor(x[:, c], w[:, c], h4[:, c], ALU.mult)
+        for c in parts:
+            nc.vector.tensor_tensor(ts[:, c], x[:, c], y[:, c], ALU.add)
+        for c in parts:
+            nc.vector.scalar_tensor_tensor(scaled[:, c], ts[:, c], og_t[:], rec[:, c], ALU.mult, ALU.mult)
+        for c in parts:
+            nc.vector.tensor_tensor(res[:, c], scaled[:, c], base_t[:, c], ALU.add)
+        nc.sync.dma_start(out=out[:, :M // 2], in_=res[:, :M // 2])
+        nc.scalar.dma_start(out=out[:, M // 2:], in_=res[:, M // 2:])

@@ -38,7 +38,6 @@ def tile_attend_ttriples_kernel(tc, dtab_words, dtab_scales, tab_words, tab_scal
 
         w_raw = keep.tile([P, PACK, R], F32, name="w_raw", tag="w_then_base")
         bias_t = keep.tile([P, 1], F32, name="bias_t")
-        og_t = keep.tile([P, 1], F32, name="og_t")
 
 
         def load_scales(tile, src):
@@ -57,23 +56,20 @@ def tile_attend_ttriples_kernel(tc, dtab_words, dtab_scales, tab_words, tab_scal
         nc.vector.memset(dtab_s[:].bitcast(I32), 0)
         nc.sync.dma_start(slots[:], offs)
         nc.sync.dma_start(first[:], offs2)
+        nc.sync.dma_start(second[:], offs3)
         nc.sync.dma_start(out=tab_w[:].bitcast(I32), in_=tab_words[0].bitcast(I32))
         nc.sync.dma_start(out=w_raw[:], in_=w1.rearrange("(p j) r -> p j r", j=PACK))
         load_scales(tab_s, tab_scales)
         nc.gpsimd.dma_start(out=bias_t[:], in_=bias)
-        nc.gpsimd.dma_start(out=og_t[:], in_=og)
         nc.sync.dma_start(out=dtab_w[:].bitcast(I32), in_=dtab_words[0].bitcast(I32))
         load_scales(dtab_s, dtab_scales)
-        nc.sync.dma_start(second[:], offs3)
         nc.sync.dma_start(third[:], offs4)
 
-        shifted = keep.tile([P, 1], F32, name="shifted")
-        nc.gpsimd.tensor_scalar(shifted[:], bias_t[:], 1.0, CLAMP, ALU.mult, ALU.add)
 
-        w_bf = keep.tile([P, R, PACK], BF16, name="w_bf", align_bytes=64)
+        w_bf = keep.tile([P, R, PACK], BF16, name="w_bf", tag="wbf_then_og", align_bytes=64)
         nc.scalar.copy(w_bf[:], w_raw[:].rearrange("p j r -> p r j"))
-        base_t = keep.tile([P, M], F32, name="base_t", tag="w_then_base")
-        nc.sync.dma_start(out=base_t[:], in_=base)
+        shifted = keep.tile([P, 1], F32, name="shifted", tag="w_then_base")
+        nc.scalar.activation(shifted[:], bias_t[:], ACT.Identity, bias=CLAMP)
         w_codes = keep.tile([P, R], U32, name="w_codes", align_bytes=64)
         w_scales = keep.tile([P, R], U8, name="w_scales", align_bytes=64)
 
@@ -108,6 +104,10 @@ def tile_attend_ttriples_kernel(tc, dtab_words, dtab_scales, tab_words, tab_scal
             nc.scalar.activation(lifted[:, cols], a[:], ACT.Relu, bias=shifted[:])
             nc.scalar.activation(sig[:, cols], lifted[:, cols], ACT.Sigmoid, bias=-CLAMP)
 
+        og_t = keep.tile([P, 1], F32, name="og_t", tag="wbf_then_og", align_bytes=64)
+        nc.sync.dma_start(out=og_t[:], in_=og)
+        base_t = keep.tile([P, M], F32, name="base_t", tag="w_then_base")
+        nc.sync.dma_start(out=base_t[:], in_=base)
         dtab_wg = gather_words("dtab_wg", dtab_w)
         tas = [product("ta%d" % half, dtab_wg, gather_scales("dtab_sg%d" % half, dtab_s, half), half) for half in range(2)]
         th = keep.tile([P, J], F32, name="th")

from contextlib import ExitStack

import concourse.mybir as mybir

F32 = mybir.dt.float32
BF16 = mybir.dt.bfloat16
I32 = mybir.dt.int32
U32 = mybir.dt.uint32
U16 = mybir.dt.uint16
U8 = mybir.dt.uint8
FP8X4 = mybir.dt.float8_e4m3fn_x4
FP4X4 = mybir.dt.float4_e2m1fn_x4
ACT = mybir.ActivationFunctionType
ALU = mybir.AluOpType

K, R, T, J, M = 512, 128, 2048, 512, 256
P = 128
PACK = 4
HALF = J // 2
CLAMP = 24.0
PARTS = 4
FLOPS = 2 * 2 * K * R * J


def tile_attend_ttriples_kernel(tc, dtab_words, dtab_scales, tab_words, tab_scales, w1, bias, og, base,
                                 offs, offs2, offs3, offs4, out):
    nc = tc.nc
    with ExitStack() as ctx:
        keep = ctx.enter_context(tc.tile_pool(name="keep", bufs=1))
        psum = ctx.enter_context(tc.psum_pool(name="psum", bufs=1))

        slots = keep.tile([P, J // 16], U16, name="slots")
        first = keep.tile([P, M // 16], U16, name="first")
        second = keep.tile([P, M // 16], U16, name="second")
        third = keep.tile([P, M // 16], U16, name="third")
        tab_s = keep.tile([P, T], U8, name="tab_s", align_bytes=64)
        tab_w = keep.tile([P, T], U16, name="tab_w", align_bytes=64)

        w_raw = keep.tile([P, PACK, R], F32, name="w_raw", tag="w_then_base")
        bias_t = keep.tile([P, 1], F32, name="bias_t")


        def load_scales(tile, src):
            rows = src[0].bitcast(I32).rearrange("(q r) c -> r q c", r=PACK)
            view = tile[:].bitcast(I32)
            for r in range(PACK):
                nc.sync.dma_start(out=view[r:P:32, :], in_=rows[r])

        nc.vector.memset(tab_s[:].bitcast(I32), 0)
        warm_in = keep.tile([P, 1], F32, name="warm_in", tag="warm_then_dtab", align_bytes=64)
        warm_out = keep.tile([P, 1], F32, name="warm_out", tag="warm_then_dscales", align_bytes=64)
        nc.gpsimd.memset(warm_in[:], 0.0)
        nc.scalar.activation(warm_out[:], warm_in[:], ACT.Sigmoid)
        dtab_w = keep.tile([P, T], U16, name="dtab_w", tag="warm_then_dtab", align_bytes=64)
        dtab_s = keep.tile([P, T], U8, name="dtab_s", tag="warm_then_dscales", align_bytes=64)
        nc.vector.memset(dtab_s[:].bitcast(I32), 0)
        nc.sync.dma_start(slots[:], offs)
        nc.sync.dma_start(first[:], offs2)
        nc.sync.dma_start(second[:], offs3)
        nc.sync.dma_start(out=tab_w[:].bitcast(I32), in_=tab_words[0].bitcast(I32))
        nc.sync.dma_start(out=w_raw[:], in_=w1.rearrange("(p j) r -> p j r", j=PACK))
        load_scales(tab_s, tab_scales)
        nc.gpsimd.dma_start(out=bias_t[:], in_=bias)
        nc.sync.dma_start(out=dtab_w[:].bitcast(I32), in_=dtab_words[0].bitcast(I32))
        load_scales(dtab_s, dtab_scales)
        nc.sync.dma_start(third[:], offs4)


        w_bf = keep.tile([P, R, PACK], BF16, name="w_bf", tag="wbf_then_og", align_bytes=64)
        nc.scalar.copy(w_bf[:], w_raw[:].rearrange("p j r -> p r j"))
        shifted = keep.tile([P, 1], F32, name="shifted", tag="w_then_base")
        nc.scalar.activation(shifted[:], bias_t[:], ACT.Identity, bias=CLAMP)
        w_codes = keep.tile([P, R], U32, name="w_codes", align_bytes=64)
        w_scales = keep.tile([P, R], U8, name="w_scales", align_bytes=64)

        def gather_words(name, window):
            g = keep.tile([P, J], U16, name=name, tag=name, align_bytes=64)
            nc.vector.tensor_copy(g[:], window[:].indirect(slots[:]))
            return g

        def gather_scales(name, window, half):
            g = keep.tile([P, HALF], U8, name=name, align_bytes=64)
            c = HALF // 16
            nc.vector.tensor_copy(g[:], window[:].indirect(slots[:, half * c:(half + 1) * c]))
            return g

        def product(name, words, scales, half):
            acc = psum.tile([P, HALF], F32, name=name)
            nc.tensor.matmul_mx(out=acc[:], lhsT=w_codes[:].bitcast(FP8X4), lhsT_scale=w_scales[:],
                                rhs=words[:, half * HALF:(half + 1) * HALF].bitcast(FP4X4), rhs_scale=scales[:],
                                start=True, stop=True)
            return acc

        tab_wg = gather_words("tab_wg", tab_w)
        tab_sg0 = gather_scales("tab_sg0", tab_s, 0)
        nc.vector.quantize_mx(out=w_codes[:].bitcast(FP8X4), scales=w_scales[:],
                              in_=w_bf[:].rearrange("p r j -> p (r j)"))
        tab_sg = [tab_sg0, gather_scales("tab_sg1", tab_s, 1)]
        lifted = keep.tile([P, J], F32, name="lifted")
        sig = keep.tile([P, J], F32, name="sig")
        for half in range(2):
            cols = slice(half * HALF, (half + 1) * HALF)
            a = product("a%d" % half, tab_wg, tab_sg[half], half)
            nc.scalar.activation(lifted[:, cols], a[:], ACT.Relu, bias=shifted[:])
            nc.scalar.activation(sig[:, cols], lifted[:, cols], ACT.Sigmoid, bias=-CLAMP)

        og_t = keep.tile([P, 1], F32, name="og_t", tag="wbf_then_og", align_bytes=64)
        nc.sync.dma_start(out=og_t[:], in_=og)
        base_t = keep.tile([P, M], F32, name="base_t", tag="w_then_base")
        nc.sync.dma_start(out=base_t[:], in_=base)
        dtab_wg = gather_words("dtab_wg", dtab_w)
        tas = [product("ta%d" % half, dtab_wg, gather_scales("dtab_sg%d" % half, dtab_s, half), half) for half in range(2)]
        th = keep.tile([P, J], F32, name="th")
        for half in range(2):
            cols = slice(half * HALF, (half + 1) * HALF)
            nc.vector.tensor_tensor(th[:, cols], tas[half][:], sig[:, cols], ALU.mult)

        logsig = keep.tile([P, J], F32, name="logsig")
        h = keep.tile([P, J], F32, name="h", tag="dtab_wg", align_bytes=64)
        for half in range(2):
            cols = slice(half * HALF, (half + 1) * HALF)
            nc.scalar.activation(logsig[:, cols], sig[:, cols], ACT.Ln)
            nc.vector.scalar_tensor_tensor(h[:, cols], lifted[:, cols], -CLAMP, logsig[:, cols], ALU.add, ALU.subtract)

        def fresh(name):
            return keep.tile([P, M], F32, name=name)

        def times(name, window, offsets, other):
            o = fresh(name)
            nc.vector.tensor_tensor(o[:], window[:].indirect(offsets[:]), other[:], ALU.mult)
            return o

        h2 = fresh("h2")
        nc.vector.tensor_copy(h2[:], h[:].indirect(first[:]))
        h3 = fresh("h3")
        nc.vector.tensor_copy(h3[:], h[:].indirect(second[:]))
        v = times("v", th, second, h2)
        pair = fresh("pair")
        nc.vector.tensor_tensor(pair[:], h2[:], h3[:], ALU.mult)
        h4 = fresh("h4")
        nc.vector.tensor_copy(h4[:], h[:].indirect(third[:]))
        u = times("u", th, first, h3)
        s = fresh("s")
        nc.vector.tensor_tensor(s[:], pair[:], h4[:], ALU.mult)
        root = fresh("root")
        rec = fresh("rec")
        nc.scalar.activation(root[:], s[:], ACT.Abs_reciprocal_sqrt, bias=1.0)
        nc.scalar.activation(rec[:], root[:], ACT.Square)
        w = fresh("w")
        nc.vector.tensor_tensor(w[:], u[:], v[:], ALU.add)
        y = times("y", th, third, pair)
        x = fresh("x")
        ts = fresh("ts")
        scaled = fresh("scaled")
        res = fresh("res")
        parts = [slice(q * M // PARTS, (q + 1) * M // PARTS) for q in range(PARTS)]
        for c in parts:
            nc.vector.tensor_tensor(x[:, c], w[:, c], h4[:, c], ALU.mult)
        for c in parts:
            nc.vector.tensor_tensor(ts[:, c], x[:, c], y[:, c], ALU.add)
        for c in parts:
            nc.vector.scalar_tensor_tensor(scaled[:, c], ts[:, c], og_t[:], rec[:, c], ALU.mult, ALU.mult)
        for c in parts:
            nc.vector.tensor_tensor(res[:, c], scaled[:, c], base_t[:, c], ALU.add)
        nc.sync.dma_start(out=out[:, :M // 2], in_=res[:, :M // 2])
        nc.scalar.dma_start(out=out[:, M // 2:], in_=res[:, M // 2:])
